import numpy as np
import ml_dtypes


def mxq(x, axis, fmt="e4m3"):
    dtype, down = {"e4m3": (ml_dtypes.float8_e4m3fn, 7), "e5m2": (ml_dtypes.float8_e5m2, 14)}[fmt]
    v = np.moveaxis(np.asarray(x, np.float32).astype(ml_dtypes.bfloat16).astype(np.float64), axis, -1)
    blocks = v.reshape(v.shape[:-1] + (-1, 32))
    amax = np.abs(blocks).max(-1, keepdims=True)
    byte = np.maximum(np.where(amax > 0, np.frexp(amax)[1] - 1 + 127, 0) - down, 1)
    scale = np.exp2(byte - 127.0)
    codes = (blocks / scale).astype(np.float32).astype(dtype).astype(np.float64)
    return np.moveaxis((codes * scale).reshape(v.shape), -1, axis)


WIDE = False


def mx_kscale(k):
    if not WIDE:
        return np.ones(k)
    levels = np.array([10, -10, 5, -5, 0])
    if k % 512:
        return np.exp2(np.random.permutation(np.resize(levels, k // 32))).repeat(32)
    a = np.empty((k // 512, 16))
    for p in range(k // 512):
        a[p, :8] = np.random.permutation(np.resize(levels, 8))
        for g in range(8):
            far = levels[np.abs(levels - a[p, g]) >= 10]
            a[p, g + 8] = far[np.random.randint(len(far))]
    return np.exp2(a.ravel()).repeat(32)


def f64(x):
    return np.asarray(x).astype(np.float64)


def striped(idx):
    return np.tile(idx.reshape(-1, 16).T, (8, 1)).astype(np.uint16)


def unstriped(offs):
    return offs[:16].T.reshape(-1).astype(np.int64)


def pack_weight(w):
    k, n = w.shape
    w = f64(np.asarray(w, np.float32).astype(ml_dtypes.bfloat16)).reshape(k // 32, 32, n)
    amax = np.abs(w).max(1)
    byte = np.clip(np.where(amax > 0, np.frexp(amax)[1] - 1 + 127 - 7, 1), 1, 254)
    scaled = (w * np.exp2(127.0 - byte)[:, None, :]).reshape(k, n).astype(np.float32)
    words = np.ascontiguousarray(scaled.reshape(k // 512, 128, 4, n).transpose(0, 1, 3, 2)).astype(ml_dtypes.float8_e4m3fn).view(np.uint8)
    return words, np.ascontiguousarray(byte.astype(np.uint8).reshape(k // 512, 16, n))


def unpack_weight(words, scales):
    g, p, n, _ = words.shape
    vals = np.ascontiguousarray(words).view(ml_dtypes.float8_e4m3fn).astype(np.float64) * np.repeat(np.exp2(scales.astype(np.float64) - 127.0), 8, axis=1)[..., None]
    return vals.transpose(0, 1, 3, 2).reshape(g * 512, n)


def silu(v):
    return v / (1.0 + np.exp(-np.maximum(v, -700.0)))


K, T, E, C, N = 1024, 2048, 16, 256, 128


def by_expert(wq, xq):
    return np.concatenate([wq[e].T @ xq[:, e * C:(e + 1) * C] for e in range(E)], axis=1)


def setup_inputs():
    n = np.random.standard_normal
    s = mx_kscale(K)[:, None]
    first = np.random.permutation(np.repeat(np.arange(E), T // E))
    second = (first + 1 + np.random.permutation(np.repeat(np.arange(E - 1), -(-T // (E - 1)))[:T])) % E
    while np.bincount(second, minlength=E).max() != T // E:
        load = np.bincount(second, minlength=E); hi, lo = int(load.argmax()), int(load.argmin())
        t = np.flatnonzero((second == hi) & (first != lo))[0]; second[t] = lo
    slot_token = np.empty(E * C, np.int64); pos = np.empty((2, T), np.int64); fill = np.zeros(E, np.int64)
    place = np.stack([np.random.permutation(C) for _ in range(E)])
    for r, deal in enumerate((first, second)):
        for t in np.random.permutation(T):
            e = deal[t]; j = e * C + place[e, fill[e]]; fill[e] += 1; slot_token[j] = t; pos[r, t] = j
    g = np.random.uniform(0.2, 0.8, T)
    packed = [pack_weight(m) for m in n((E, K, N)) / np.sqrt(K) / s[None]]
    return {
        "xT": (n((K, T)) * s).astype(np.float32),
        "w_words": np.stack([m[0] for m in packed]),
        "w_scales": np.stack([m[1] for m in packed]),
        "b": (0.3 * n((N, E))).astype(np.float32),
        "gate": np.stack([np.tile(g, (N, 1)), np.tile(1.0 - g, (N, 1))]).astype(np.float32),
        "offs": striped(slot_token),
        "pos1": striped(pos[0]),
        "pos2": striped(pos[1]),
    }


def reference(xT, w_words, w_scales, b, gate, offs, pos1, pos2):
    idx = unstriped(offs)
    xq = mxq(f64(xT)[:, idx], 0, "e4m3")
    w = np.stack([unpack_weight(w_words[e], w_scales[e]) for e in range(E)])
    y = by_expert(w, xq)
    y = silu(y + np.repeat(f64(b), C, axis=1))
    return f64(gate[0]) * y[:, unstriped(pos1)] + f64(gate[1]) * y[:, unstriped(pos2)]

@@ -1,0 +1,163 @@
+from contextlib import ExitStack
+
+import concourse.mybir as mybir
+from concourse.masks import make_identity
+
+K, T, E, C, N = 1024, 2048, 16, 256, 128
+P = 128
+PASSES = 2
+SLOTS = E * C
+FLOPS = 2 * SLOTS * K * N
+
+F32 = mybir.dt.float32
+BF16 = mybir.dt.bfloat16
+I32 = mybir.dt.int32
+U32 = mybir.dt.uint32
+U16 = mybir.dt.uint16
+U8 = mybir.dt.uint8
+FP8X4 = mybir.dt.float8_e4m3fn_x4
+MULT = mybir.AluOpType.mult
+SILU = mybir.ActivationFunctionType.Silu
+
+CHUNKS = (
+    ((512, 320), (512, 320), (512, 320), (256, 160), (256, 160)),
+    ((512, 0), (512, 0), (512, 0), (256, 0), (256, 160)),
+)
+WORD0_CUTS = (1536, 1536, 1024)
+SCALE_CUTS = (1536, 1536, 1024)
+WORD1_CUTS = (1536, 1536, 768, 256)
+OUT_CUTS = ((512, True), (512, True), (512, True), (256, False), (256, False))
+
+
+def tile_routed_moe_kernel(tc, xT, w_words, w_scales, b, gate, offs, pos1, pos2, out):
+    nc = tc.nc
+    with ExitStack() as ctx:
+        lists = ctx.enter_context(tc.tile_pool(name="lists", bufs=1))
+        keep = ctx.enter_context(tc.tile_pool(name="keep", bufs=1))
+        raws = ctx.enter_context(tc.tile_pool(name="raws", bufs=8))
+        grouped = ctx.enter_context(tc.tile_pool(name="grouped", bufs=4))
+        psum = ctx.enter_context(tc.psum_pool(name="psum", bufs=4))
+
+        offs_sb = lists.tile([P, SLOTS // 16], U16, name="offs_sb")
+        pos1_sb = lists.tile([P, T // 16], U16, name="pos1_sb")
+        pos2_sb = lists.tile([P, T // 16], U16, name="pos2_sb")
+
+        words = [keep.tile([P, T], U32, name="words%d" % a, align_bytes=64) for a in range(PASSES)]
+        scales = keep.tile([P, T], U8, name="scales", align_bytes=64)
+        slot_words = [keep.tile([P, SLOTS], U32, name="slot_words%d" % a, align_bytes=64) for a in range(PASSES)]
+        slot_scales = keep.tile([P, SLOTS], U8, name="slot_scales", align_bytes=64)
+        w_sb = keep.tile([P, E, PASSES, N], I32, name="w_sb", align_bytes=64)
+        ws_sb = keep.tile([P, E, N], U8, name="ws_sb", align_bytes=64)
+        b_sb = keep.tile([P, E], F32, name="b_sb")
+        gate_sb = [keep.tile([P, T], F32, name="gate_sb%d" % r) for r in range(2)]
+        y = keep.tile([P, SLOTS], F32, name="y")
+
+        ident = keep.tile([P, P], F32, name="ident")
+        nc.gpsimd.memset(scales[:], 0)
+        nc.gpsimd.memset(ws_sb[:], 0)
+        make_identity(nc, ident[:])
+
+        def load(a):
+            got = []
+            t0 = 0
+            rows = xT[a * 512 : (a + 1) * 512, :].rearrange("(p j) t -> p j t", j=4)
+            for n, v in CHUNKS[a]:
+                raw = raws.tile([P, 4, n], F32, name="raw")
+                nc.sync.dma_start(out=raw[:], in_=rows[:, :, t0 : t0 + n])
+                got.append((raw, t0, n, v))
+                t0 += n
+            return got
+
+        def quantise(a, chunk):
+            raw, t0, n, v = chunk
+            g = grouped.tile([P, n, 4], BF16, name="g", align_bytes=64)
+            nc.scalar.copy(out=g[:, v:n, :], in_=raw[:, :, v:n].rearrange("p j t -> p t j"))
+            if v:
+                nc.vector.tensor_copy(out=g[:, 0:v, :], in_=raw[:, :, 0:v].rearrange("p j t -> p t j"))
+            nc.vector.quantize_mx(
+                out=words[a][:, t0 : t0 + n].bitcast(FP8X4),
+                scales=scales[4 * a : P, t0 : t0 + n],
+                in_=g[:].rearrange("p t j -> p (t j)"),
+            )
+
+        def gather_words(a, s0, n):
+            cols = slice(s0, s0 + n)
+            nc.vector.tensor_copy(slot_words[a][:, cols], words[a][:].indirect(offs_sb[:, s0 // 16 : (s0 + n) // 16]))
+
+        def gather_scales(s0, n):
+            cols = slice(s0, s0 + n)
+            nc.vector.tensor_copy(slot_scales[:, cols], scales[:].indirect(offs_sb[:, s0 // 16 : (s0 + n) // 16]))
+
+        def expert(e):
+            cols = slice(e * C, (e + 1) * C)
+            acc = psum.tile([P, C], F32, name="acc")
+            for a in range(PASSES):
+                nc.tensor.matmul_mx(
+                    out=acc[:],
+                    lhsT=w_sb[:, e, a, :].bitcast(FP8X4),
+                    lhsT_scale=ws_sb[4 * a : P, e, :],
+                    rhs=slot_words[a][:, cols].bitcast(FP8X4),
+                    rhs_scale=slot_scales[4 * a : P, cols],
+                    start=(a == 0),
+                    stop=(a == PASSES - 1),
+                )
+            nc.scalar.activation(out=y[:, cols], in_=acc[:], func=SILU, bias=b_sb[:, e : e + 1])
+
+        chunks0 = load(0)
+        nc.sync.dma_start(offs_sb[:], offs)
+        chunks1 = load(1)
+        for a in range(PASSES):
+            for q in range(4):
+                nc.sync.dma_start(
+                    out=ws_sb[32 * q + 4 * a : 32 * q + 4 * a + 4, :, :].bitcast(I32),
+                    in_=w_scales[:, a, 4 * q : 4 * q + 4, :].rearrange("e q n -> q e n").bitcast(I32),
+                )
+        for h in range(2):
+            es = slice(h * E // 2, (h + 1) * E // 2)
+            nc.sync.dma_start(
+                out=w_sb[:, es, :, :].rearrange("p e a n -> p (e a) n"),
+                in_=w_words[es].rearrange("e a p n r -> p (e a) (n r)").bitcast(I32),
+            )
+        nc.sync.dma_start(b_sb[:], b)
+        nc.sync.dma_start(pos1_sb[:], pos1)
+        nc.sync.dma_start(pos2_sb[:], pos2)
+        for r in range(2):
+            nc.sync.dma_start(gate_sb[r][:], gate[r])
+
+        for chunk in chunks0:
+            quantise(0, chunk)
+        s0 = 0
+        for n in WORD0_CUTS:
+            gather_words(0, s0, n)
+            s0 += n
+        for chunk in chunks1:
+            quantise(1, chunk)
+        s0 = 0
+        for n in SCALE_CUTS:
+            gather_scales(s0, n)
+            s0 += n
+        s0 = 0
+        for n in WORD1_CUTS:
+            gather_words(1, s0, n)
+            for e in range(s0 // C, (s0 + n) // C):
+                expert(e)
+            s0 += n
+
+        t0 = 0
+        for i, (n, on_tensor) in enumerate(OUT_CUTS):
+            cols = slice(t0, t0 + n)
+            at = slice(t0 // 16, (t0 + n) // 16)
+            u = keep.tile([P, n], F32, name="u%d" % i)
+            v = keep.tile([P, n], F32, name="v%d" % i)
+            o = keep.tile([P, n], F32, name="o%d" % i)
+            nc.vector.tensor_tensor(u[:], y[:].indirect(pos1_sb[:, at]), gate_sb[0][:, cols], MULT)
+            nc.vector.tensor_tensor(v[:], y[:].indirect(pos2_sb[:, at]), gate_sb[1][:, cols], MULT)
+            if on_tensor:
+                both = psum.tile([P, n], F32, name="both")
+                nc.tensor.matmul(both[:], ident[:], u[:], start=True, stop=False)
+                nc.tensor.matmul(both[:], ident[:], v[:], start=False, stop=True)
+                nc.scalar.copy(out=o[:], in_=both[:])
+            else:
+                nc.vector.tensor_add(out=o[:], in0=u[:], in1=v[:])
+            nc.sync.dma_start(out=out[:, cols], in_=o[:])
+            t0 += n

@@ -20,7 +20,7 @@ MULT = mybir.AluOpType.mult
 SILU = mybir.ActivationFunctionType.Silu
 
 CHUNKS = (
-    ((512, 320), (512, 320), (512, 320), (256, 160), (256, 160)),
+    ((1024, 640), (512, 320), (256, 160), (256, 160)),
     ((512, 0), (512, 0), (512, 0), (256, 0), (256, 160)),
 )
 WORD0_CUTS = (1536, 1536, 1024)
@@ -34,7 +34,7 @@ def tile_routed_moe_kernel(tc, xT, w_words, w_scales, b, gate, offs, pos1, pos2,
     with ExitStack() as ctx:
         lists = ctx.enter_context(tc.tile_pool(name="lists", bufs=1))
         keep = ctx.enter_context(tc.tile_pool(name="keep", bufs=1))
-        raws = ctx.enter_context(tc.tile_pool(name="raws", bufs=8))
+        raws = ctx.enter_context(tc.tile_pool(name="raws", bufs=1))
         grouped = ctx.enter_context(tc.tile_pool(name="grouped", bufs=4))
         psum = ctx.enter_context(tc.psum_pool(name="psum", bufs=4))
 
@@ -62,18 +62,24 @@ def tile_routed_moe_kernel(tc, xT, w_words, w_scales, b, gate, offs, pos1, pos2,
             t0 = 0
             rows = xT[a * 512 : (a + 1) * 512, :].rearrange("(p j) t -> p j t", j=4)
             for n, v in CHUNKS[a]:
-                raw = raws.tile([P, 4, n], F32, name="raw")
+                raw = raws.tile([P, 4, n], F32, name="raw%d_%d" % (a, t0))
                 nc.sync.dma_start(out=raw[:], in_=rows[:, :, t0 : t0 + n])
                 got.append((raw, t0, n, v))
                 t0 += n
             return got
 
+        def interleave(copy, g, raw, lo, hi):
+            copy(
+                out=g[:, lo:hi, :].rearrange("p (c i) j -> p c j i", i=4),
+                in_=raw[:, :, lo:hi].rearrange("p j (c i) -> p c j i", i=4),
+            )
+
         def quantise(a, chunk):
             raw, t0, n, v = chunk
             g = grouped.tile([P, n, 4], BF16, name="g", align_bytes=64)
-            nc.scalar.copy(out=g[:, v:n, :], in_=raw[:, :, v:n].rearrange("p j t -> p t j"))
+            interleave(nc.scalar.copy, g, raw, v, n)
             if v:
-                nc.vector.tensor_copy(out=g[:, 0:v, :], in_=raw[:, :, 0:v].rearrange("p j t -> p t j"))
+                interleave(nc.vector.tensor_copy, g, raw, 0, v)
             nc.vector.quantize_mx(
                 out=words[a][:, t0 : t0 + n].bitcast(FP8X4),
                 scales=scales[4 * a : P, t0 : t0 + n],

from contextlib import ExitStack

import concourse.mybir as mybir
from concourse.masks import make_identity

K, T, E, C, N = 1024, 2048, 16, 256, 128
P = 128
PASSES = 2
SLOTS = E * C
FLOPS = 2 * SLOTS * K * N

F32 = mybir.dt.float32
BF16 = mybir.dt.bfloat16
I32 = mybir.dt.int32
U32 = mybir.dt.uint32
U16 = mybir.dt.uint16
U8 = mybir.dt.uint8
FP8X4 = mybir.dt.float8_e4m3fn_x4
MULT = mybir.AluOpType.mult
SILU = mybir.ActivationFunctionType.Silu

CHUNKS = (
    ((1024, 640), (512, 320), (256, 160), (256, 160)),
    ((512, 0), (512, 0), (512, 0), (256, 0), (256, 160)),
)
WORD0_CUTS = (1536, 1536, 1024)
SCALE_CUTS = (1536, 1536, 1024)
WORD1_CUTS = (1536, 1536, 768, 256)
OUT_CUTS = ((512, True), (512, True), (512, True), (256, False), (256, False))


def tile_routed_moe_kernel(tc, xT, w_words, w_scales, b, gate, offs, pos1, pos2, out):
    nc = tc.nc
    with ExitStack() as ctx:
        lists = ctx.enter_context(tc.tile_pool(name="lists", bufs=1))
        keep = ctx.enter_context(tc.tile_pool(name="keep", bufs=1))
        raws = ctx.enter_context(tc.tile_pool(name="raws", bufs=1))
        grouped = ctx.enter_context(tc.tile_pool(name="grouped", bufs=4))
        psum = ctx.enter_context(tc.psum_pool(name="psum", bufs=4))

        offs_sb = lists.tile([P, SLOTS // 16], U16, name="offs_sb")
        pos1_sb = lists.tile([P, T // 16], U16, name="pos1_sb")
        pos2_sb = lists.tile([P, T // 16], U16, name="pos2_sb")

        words = [keep.tile([P, T], U32, name="words%d" % a, align_bytes=64) for a in range(PASSES)]
        scales = keep.tile([P, T], U8, name="scales", align_bytes=64)
        slot_words = [keep.tile([P, SLOTS], U32, name="slot_words%d" % a, align_bytes=64) for a in range(PASSES)]
        slot_scales = keep.tile([P, SLOTS], U8, name="slot_scales", align_bytes=64)
        w_sb = keep.tile([P, E, PASSES, N], I32, name="w_sb", align_bytes=64)
        ws_sb = keep.tile([P, E, N], U8, name="ws_sb", align_bytes=64)
        b_sb = keep.tile([P, E], F32, name="b_sb")
        gate_sb = [keep.tile([P, T], F32, name="gate_sb%d" % r) for r in range(2)]
        y = keep.tile([P, SLOTS], F32, name="y")

        ident = keep.tile([P, P], F32, name="ident")
        nc.gpsimd.memset(scales[:], 0)
        nc.gpsimd.memset(ws_sb[:], 0)
        make_identity(nc, ident[:])

        def load(a):
            got = []
            t0 = 0
            rows = xT[a * 512 : (a + 1) * 512, :].rearrange("(p j) t -> p j t", j=4)
            for n, v in CHUNKS[a]:
                raw = raws.tile([P, 4, n], F32, name="raw%d_%d" % (a, t0))
                nc.sync.dma_start(out=raw[:], in_=rows[:, :, t0 : t0 + n])
                got.append((raw, t0, n, v))
                t0 += n
            return got

        def interleave(copy, g, raw, lo, hi):
            copy(
                out=g[:, lo:hi, :].rearrange("p (c i) j -> p c j i", i=4),
                in_=raw[:, :, lo:hi].rearrange("p j (c i) -> p c j i", i=4),
            )

        def quantise(a, chunk):
            raw, t0, n, v = chunk
            g = grouped.tile([P, n, 4], BF16, name="g", align_bytes=64)
            interleave(nc.scalar.copy, g, raw, v, n)
            if v:
                interleave(nc.vector.tensor_copy, g, raw, 0, v)
            nc.vector.quantize_mx(
                out=words[a][:, t0 : t0 + n].bitcast(FP8X4),
                scales=scales[4 * a : P, t0 : t0 + n],
                in_=g[:].rearrange("p t j -> p (t j)"),
            )

        def gather_words(a, s0, n):
            cols = slice(s0, s0 + n)
            nc.vector.tensor_copy(slot_words[a][:, cols], words[a][:].indirect(offs_sb[:, s0 // 16 : (s0 + n) // 16]))

        def gather_scales(s0, n):
            cols = slice(s0, s0 + n)
            nc.vector.tensor_copy(slot_scales[:, cols], scales[:].indirect(offs_sb[:, s0 // 16 : (s0 + n) // 16]))

        def expert(e):
            cols = slice(e * C, (e + 1) * C)
            acc = psum.tile([P, C], F32, name="acc")
            for a in range(PASSES):
                nc.tensor.matmul_mx(
                    out=acc[:],
                    lhsT=w_sb[:, e, a, :].bitcast(FP8X4),
                    lhsT_scale=ws_sb[4 * a : P, e, :],
                    rhs=slot_words[a][:, cols].bitcast(FP8X4),
                    rhs_scale=slot_scales[4 * a : P, cols],
                    start=(a == 0),
                    stop=(a == PASSES - 1),
                )
            nc.scalar.activation(out=y[:, cols], in_=acc[:], func=SILU, bias=b_sb[:, e : e + 1])

        chunks0 = load(0)
        nc.sync.dma_start(offs_sb[:], offs)
        chunks1 = load(1)
        for a in range(PASSES):
            for q in range(4):
                nc.sync.dma_start(
                    out=ws_sb[32 * q + 4 * a : 32 * q + 4 * a + 4, :, :].bitcast(I32),
                    in_=w_scales[:, a, 4 * q : 4 * q + 4, :].rearrange("e q n -> q e n").bitcast(I32),
                )
        for h in range(2):
            es = slice(h * E // 2, (h + 1) * E // 2)
            nc.sync.dma_start(
                out=w_sb[:, es, :, :].rearrange("p e a n -> p (e a) n"),
                in_=w_words[es].rearrange("e a p n r -> p (e a) (n r)").bitcast(I32),
            )
        nc.sync.dma_start(b_sb[:], b)
        nc.sync.dma_start(pos1_sb[:], pos1)
        nc.sync.dma_start(pos2_sb[:], pos2)
        for r in range(2):
            nc.sync.dma_start(gate_sb[r][:], gate[r])

        for chunk in chunks0:
            quantise(0, chunk)
        s0 = 0
        for n in WORD0_CUTS:
            gather_words(0, s0, n)
            s0 += n
        for chunk in chunks1:
            quantise(1, chunk)
        s0 = 0
        for n in SCALE_CUTS:
            gather_scales(s0, n)
            s0 += n
        s0 = 0
        for n in WORD1_CUTS:
            gather_words(1, s0, n)
            for e in range(s0 // C, (s0 + n) // C):
                expert(e)
            s0 += n

        t0 = 0
        for i, (n, on_tensor) in enumerate(OUT_CUTS):
            cols = slice(t0, t0 + n)
            at = slice(t0 // 16, (t0 + n) // 16)
            u = keep.tile([P, n], F32, name="u%d" % i)
            v = keep.tile([P, n], F32, name="v%d" % i)
            o = keep.tile([P, n], F32, name="o%d" % i)
            nc.vector.tensor_tensor(u[:], y[:].indirect(pos1_sb[:, at]), gate_sb[0][:, cols], MULT)
            nc.vector.tensor_tensor(v[:], y[:].indirect(pos2_sb[:, at]), gate_sb[1][:, cols], MULT)
            if on_tensor:
                both = psum.tile([P, n], F32, name="both")
                nc.tensor.matmul(both[:], ident[:], u[:], start=True, stop=False)
                nc.tensor.matmul(both[:], ident[:], v[:], start=False, stop=True)
                nc.scalar.copy(out=o[:], in_=both[:])
            else:
                nc.vector.tensor_add(out=o[:], in0=u[:], in1=v[:])
            nc.sync.dma_start(out=out[:, cols], in_=o[:])
            t0 += n
